import numpy as np
import ml_dtypes


def mxq(x, axis, fmt="e4m3"):
    dtype, down = {"e4m3": (ml_dtypes.float8_e4m3fn, 7), "e5m2": (ml_dtypes.float8_e5m2, 14)}[fmt]
    v = np.moveaxis(np.asarray(x, np.float32).astype(ml_dtypes.bfloat16).astype(np.float64), axis, -1)
    blocks = v.reshape(v.shape[:-1] + (-1, 32))
    amax = np.abs(blocks).max(-1, keepdims=True)
    byte = np.maximum(np.where(amax > 0, np.frexp(amax)[1] - 1 + 127, 0) - down, 1)
    scale = np.exp2(byte - 127.0)
    codes = (blocks / scale).astype(np.float32).astype(dtype).astype(np.float64)
    return np.moveaxis((codes * scale).reshape(v.shape), -1, axis)


WIDE = False


def mx_kscale(k):
    if not WIDE:
        return np.ones(k)
    levels = np.array([10, -10, 5, -5, 0])
    if k % 512:
        return np.exp2(np.random.permutation(np.resize(levels, k // 32))).repeat(32)
    a = np.empty((k // 512, 16))
    for p in range(k // 512):
        a[p, :8] = np.random.permutation(np.resize(levels, 8))
        for g in range(8):
            far = levels[np.abs(levels - a[p, g]) >= 10]
            a[p, g + 8] = far[np.random.randint(len(far))]
    return np.exp2(a.ravel()).repeat(32)


def f64(x):
    return np.asarray(x).astype(np.float64)


def striped(idx):
    return np.tile(np.asarray(idx).reshape(-1, 16).T, (8, 1)).astype(np.uint16)


def unstriped(offs):
    return offs[:16].T.reshape(-1).astype(np.int64)


def striped8(idx):
    return np.asarray(idx).reshape(8, -1, 16).transpose(0, 2, 1).reshape(128, -1).astype(np.uint16)


def unstriped8(offs):
    return offs.reshape(8, 16, -1).transpose(0, 2, 1).reshape(8, -1).astype(np.int64)


def pick8(x, idx, run):
    r = np.arange(len(x))
    return x[r[:, None], idx[r % (8 * run) // run]]


E2M1 = np.array([0.0, 0.5, 1.0, 1.5, 2.0, 3.0, 4.0, 6.0, -0.0, -0.5, -1.0, -1.5, -2.0, -3.0, -4.0, -6.0])


def pack_weight(w, fmt):
    k, n = w.shape
    w = f64(np.asarray(w, np.float32).astype(ml_dtypes.bfloat16)).reshape(k // 32, 32, n)
    amax = np.abs(w).max(1)
    if fmt == "e4m3":
        byte = np.frexp(amax)[1] - 1 + 127 - 7
    else:
        mant, ex = np.frexp(amax / 6.0)
        byte = np.where(mant > 0.5, ex, ex - 1) + 127
    byte = np.clip(np.where(amax > 0, byte, 1), 1, 254)
    scaled = (w * np.exp2(127.0 - byte)[:, None, :]).reshape(k, n).astype(np.float32)
    by_word = np.ascontiguousarray(scaled.reshape(k // 512, 128, 4, n).transpose(0, 1, 3, 2))
    if fmt == "e4m3":
        words = by_word.astype(ml_dtypes.float8_e4m3fn).view(np.uint8)
    else:
        c = by_word.astype(ml_dtypes.float4_e2m1fn).view(np.uint8) & 0xF
        words = (c[..., 0::2] | (c[..., 1::2] << 4)).reshape(k // 512, 128, 2 * n)
    return np.ascontiguousarray(words), np.ascontiguousarray(byte.astype(np.uint8).reshape(k // 512, 16, n))


def unpack_weight(words, scales, fmt):
    g, _, n = scales.shape
    words = np.ascontiguousarray(words).reshape(g, 128, n, -1)
    if fmt == "e4m3":
        vals = words.view(ml_dtypes.float8_e4m3fn).astype(np.float64)
    else:
        nib = np.empty((g, 128, n, 4), np.uint8)
        nib[..., 0::2] = words & 0xF
        nib[..., 1::2] = words >> 4
        vals = E2M1[nib]
    vals = vals * np.repeat(np.exp2(scales.astype(np.float64) - 127.0), 8, axis=1)[..., None]
    return vals.transpose(0, 1, 3, 2).reshape(g * 512, n)


def sgn(shape):
    return np.random.uniform(0.5, 2.0, shape) * np.where(np.random.standard_normal(shape) < 0, -1.0, 1.0)


K, J, R, T, F, G, O, N, U, E = 512, 512, 512, 2048, 2048, 1024, 256, 256, 128, 512


def setup_inputs():
    n = np.random.standard_normal
    idx = np.random.permutation(T)[:J]
    idx2 = np.stack([np.random.permutation(F)[:G] for _ in range(8)])
    idx3 = np.random.permutation(G)[:R]
    idx4 = np.random.permutation(J)[:O]
    idx5 = np.stack([np.random.permutation(J)[:O] for _ in range(8)])
    idx6 = np.stack([np.random.permutation(O)[:U] for _ in range(8)])
    idx7 = np.stack([np.random.permutation(E)[:U] for _ in range(8)])
    fk = mx_kscale(K)
    fr = mx_kscale(R)
    xtp = pack_weight(n((K, T)) * fk[:, None], "e2m1")
    wbp = pack_weight(n((R, N)) * 1 / np.sqrt(R) / fr[:, None], "e2m1")
    return {
        "xt_words": xtp[0],
        "xt_scales": xtp[1],
        "ua": (np.random.randint(-7, 8, (K, F)).astype(np.float64)).astype(np.float32),
        "ha": ((np.random.randint(8, 25, (K, 1)) / 1024.0) / fk[:, None]).astype(np.float32),
        "hb": (np.random.uniform(0.5, 1.6, (K, 1))).astype(np.float32),
        "sa": (np.random.uniform(0.5, 1.6, (R, 1)) * fr[:, None]).astype(np.float32),
        "sb": (np.random.uniform(0.5, 1.6, (R, 1)) * fr[:, None]).astype(np.float32),
        "wb_words": wbp[0],
        "wb_scales": wbp[1],
        "so": (sgn((N, 1))).astype(np.float32),
        "offs": striped(idx),
        "offs2": striped8(idx2),
        "offs3": striped(idx3),
        "offs4": striped(idx4),
        "offs5": striped8(idx5),
        "offs6": striped8(idx6),
        "offs7": striped8(idx7),
    }


def reference(xt_words, xt_scales, ua, ha, hb, sa, sb, wb_words, wb_scales, so, offs, offs2, offs3, offs4, offs5, offs6, offs7):
    idx = unstriped(offs)
    idx2 = unstriped8(offs2)
    idx3 = unstriped(offs3)
    idx4 = unstriped(offs4)
    idx5 = unstriped8(offs5)
    idx6 = unstriped8(offs6)
    idx7 = unstriped8(offs7)
    xtu = unpack_weight(xt_words, xt_scales, "e2m1")
    wbu = unpack_weight(wb_words, wb_scales, "e2m1")
    wcd = pick8(f64(ua), idx2, 64) * f64(ha)
    wc = wcd[:, idx3] * f64(hb)
    wcq = mxq(wc, 0, "e4m3")
    xtidxg = xtu[:, idx]
    a = wcq.T @ xtidxg
    hid = np.maximum(a[:, idx4] * f64(sa), pick8(a, idx5, 64) * f64(sb))
    hidq = mxq(hid, 0, "e4m3")
    p = wbu.T @ hidq
    m0 = pick8(p, idx6, 16) * f64(so)
    y = np.zeros((N, E))
    y[np.arange(N)[:, None], idx7[np.arange(N) % 128 // 16]] = m0
    return y

@@ -1,0 +1,192 @@
+from contextlib import ExitStack
+
+import concourse.mybir as mybir
+
+K, J, R, T, F, G, O, N, U, E = 512, 512, 512, 2048, 2048, 1024, 256, 256, 128, 512
+FLOPS = 2 * K * R * J + 2 * R * N * O
+
+F32 = mybir.dt.float32
+BF16 = mybir.dt.bfloat16
+I32 = mybir.dt.int32
+U32 = mybir.dt.uint32
+U16 = mybir.dt.uint16
+U8 = mybir.dt.uint8
+FP8X4 = mybir.dt.float8_e4m3fn_x4
+FP4X4 = mybir.dt.float4_e2m1fn_x4
+COPY = mybir.ActivationFunctionType.Copy
+MAX = mybir.AluOpType.max
+
+P = 128
+PACK = 4
+LIST_ROWS = 16
+ALIGN = 64
+
+
+def tile_picked_tokens_respelled_one_mixedpair_one_posted_kernel(
+    tc, xt_words, xt_scales, ua, ha, hb, sa, sb, wb_words, wb_scales, so,
+    offs, offs2, offs3, offs4, offs5, offs6, offs7, out,
+):
+    nc = tc.nc
+    with ExitStack() as ctx:
+        lists = ctx.enter_context(tc.tile_pool(name="lists", bufs=1))
+        pool = ctx.enter_context(tc.tile_pool(name="work", bufs=1))
+        psum = ctx.enter_context(tc.psum_pool(name="psum", bufs=1))
+
+        def load_list(src, name):
+            t = lists.tile(list(src.shape), U16, name=name)
+            nc.sync.dma_start(t[:], src)
+            return t
+
+        def load_factor(queue, src, name, tag):
+            t = pool.tile([P, PACK], F32, name=name, tag=tag)
+            queue.dma_start(t[:], src.rearrange("(p t) o -> p (t o)", t=PACK))
+            return t
+
+        def load_scale_rows(dst, src):
+            for q in range(4):
+                nc.sync.dma_start(dst[32 * q:32 * q + 4, :].bitcast(I32), src[0, 4 * q:4 * q + 4, :].bitcast(I32))
+
+        def entries(lst, start, count):
+            return lst[:, start // LIST_ROWS:(start + count) // LIST_ROWS]
+
+        def fetch(dst, window, offsets, scale):
+            nc.scalar.activation(out=dst, in_=window[:].indirect(offsets), func=COPY, scale=scale)
+
+        ua_rows = ua.rearrange("(p t) f -> t p f", t=PACK)
+        ua_sb = [pool.tile([P, F], F32, name="ua%d" % t, tag="ua%d" % t) for t in range(PACK)]
+        l2 = load_list(offs2, "l2")
+        ha_sb = load_factor(nc.scalar, ha, "ha_sb", "ha_sb")
+        nc.sync.dma_start(ua_sb[0][:], ua_rows[0])
+        l3 = load_list(offs3, "l3")
+        hb_sb = load_factor(nc.scalar, hb, "hb_sb", "hb_sb")
+        for t in range(1, PACK):
+            nc.sync.dma_start(ua_sb[t][:], ua_rows[t])
+
+        xs_all = pool.tile([P, T], U8, name="xs_all", tag="xs_all", align_bytes=ALIGN)
+        nc.vector.memset(xs_all[:].bitcast(I32), 0)
+        wb_s = pool.tile([P, N], U8, name="wb_s", align_bytes=ALIGN)
+        nc.vector.memset(wb_s[:].bitcast(I32), 0)
+        pages = [pool.tile([P, E], F32, name="page%d" % b) for b in range(N // P)]
+        for page in pages:
+            nc.vector.memset(page[:], 0.0)
+
+        xw_all = pool.tile([P, T], U16, name="xw_all")
+        nc.sync.dma_start(xw_all[:].bitcast(I32), xt_words[0].bitcast(I32))
+        l1 = load_list(offs, "l1")
+        load_scale_rows(xs_all, xt_scales)
+        sa_sb = load_factor(nc.sync, sa, "sa_sb", "sa_sb")
+        l4 = load_list(offs4, "l4")
+        sb_sb = load_factor(nc.sync, sb, "sb_sb", "sb_sb")
+        l5 = load_list(offs5, "l5")
+        wb_w = pool.tile([P, N], U16, name="wb_w", align_bytes=ALIGN)
+        nc.sync.dma_start(wb_w[:].bitcast(I32), wb_words[0].bitcast(I32))
+        load_scale_rows(wb_s, wb_scales)
+        so_sb = pool.tile([P, N // P], F32, name="so_sb")
+        with nc.allow_non_contiguous_dma(reason="one weight for each output feature, one feature a partition"):
+            nc.sync.dma_start(so_sb[:], so.rearrange("(b p) o -> p (b o)", p=P))
+        l6 = load_list(offs6, "l6")
+        l7 = load_list(offs7, "l7")
+
+        xw = pool.tile([P, J], U16, name="xw", align_bytes=ALIGN)
+        nc.vector.tensor_copy(xw[:], xw_all[:].indirect(l1[:]))
+        xs = pool.tile([P, J], U8, name="xs", align_bytes=ALIGN)
+        nc.vector.tensor_copy(xs[:], xs_all[:].indirect(l1[:]))
+
+        HR = R // 2
+        HM = HR // PACK
+        wcd = [pool.tile([P, G], F32, name="wcd%d" % t) for t in range(PACK)]
+        wc_lo = pool.tile([P, PACK, HR], BF16, name="wc_lo")
+        for t in range(PACK):
+            fetch(wcd[t][:], ua_sb[t], l2[:], ha_sb[:, t:t + 1])
+            fetch(wc_lo[:, t, :], wcd[t], entries(l3, 0, HR), hb_sb[:, t:t + 1])
+        wc_hi = pool.tile([P, PACK, HR], BF16, name="wc_hi", tag="ua%d" % (PACK - 1))
+        for t in range(PACK):
+            fetch(wc_hi[:, t, :], wcd[t], entries(l3, HR, HR), hb_sb[:, t:t + 1])
+
+        wq = [pool.tile([P, P], U32, name="wq%d" % s, align_bytes=ALIGN) for s in range(PACK)]
+        wq_s = [pool.tile([P, P], U8, name="wq_s%d" % s, align_bytes=ALIGN) for s in range(PACK)]
+
+        def quantize_wc(grouped, s, half):
+            cols = slice(half * HM, (half + 1) * HM)
+            nc.vector.quantize_mx(out=wq[s][:, cols].bitcast(FP8X4), scales=wq_s[s][:, cols], in_=grouped)
+
+        g_lo = pool.tile([P, PACK, HR], BF16, name="g_lo", tag="xs_all", align_bytes=ALIGN)
+        nc.vector.tensor_copy(
+            g_lo[:].rearrange("p s (c i t) -> p c t i s", i=2, t=PACK),
+            wc_lo[:].rearrange("p t (c i s) -> p c t i s", i=2, s=PACK),
+        )
+        for s in range(PACK):
+            quantize_wc(g_lo[:, s, :], s, 0)
+
+        wc_hi_v = wc_hi[:].rearrange("p t (c i s) -> p s c t i", i=2, s=PACK)
+        g_hi = [pool.tile([P, HR], BF16, name="g_hi%d" % s, align_bytes=ALIGN) for s in range(PACK)]
+        for pair in ((0, 1), (2, 3)):
+            for s in pair:
+                nc.vector.tensor_copy(g_hi[s][:].rearrange("p (c i t) -> p c t i", i=2, t=PACK), wc_hi_v[:, s])
+            for s in pair:
+                quantize_wc(g_hi[s][:], s, 1)
+
+        def product1(acc, s, cols):
+            nc.tensor.matmul_mx(
+                out=acc, lhsT=wq[s][:].bitcast(FP8X4), lhsT_scale=wq_s[s][:],
+                rhs=xw[:, cols].bitcast(FP4X4), rhs_scale=xs[:, cols], start=True, stop=True,
+            )
+
+        a_sb = [pool.tile([P, J], F32, name="a%d" % s) for s in range(PACK)]
+        for h in range(2):
+            cols = slice(h * J // 2, (h + 1) * J // 2)
+            acc = psum.tile([P, J // 2], F32, name="acc0_%d" % h)
+            product1(acc[:], 0, cols)
+            nc.scalar.copy(a_sb[0][:, cols], acc[:])
+        for s in range(1, PACK):
+            acc = psum.tile([P, J], F32, name="acc%d" % s)
+            product1(acc[:], s, slice(0, J))
+            nc.vector.tensor_copy(a_sb[s][:], acc[:])
+
+        HO = O // 2
+        first_lo = pool.tile([P, PACK, HO], F32, name="first_lo")
+        second = pool.tile([P, PACK, O], F32, name="second")
+        for s in range(PACK):
+            fetch(first_lo[:, s, :], a_sb[s], entries(l4, 0, HO), sa_sb[:, s:s + 1])
+            fetch(second[:, s, :], a_sb[s], l5[:], sb_sb[:, s:s + 1])
+        first_hi = pool.tile([P, PACK, HO], F32, name="first_hi", tag="sb_sb")
+        for s in range(PACK):
+            fetch(first_hi[:, s, :], a_sb[s], entries(l4, HO, HO), sa_sb[:, s:s + 1])
+
+        p_sb = [pool.tile([P, O], F32, name="p%d" % b) for b in range(N // P)]
+        acc_lo = psum.tile([P, N // P, HO], F32, name="acc_lo")
+        for h, first in enumerate((first_lo, first_hi)):
+            cols = slice(h * HO, (h + 1) * HO)
+            hid = pool.tile([P, HO * PACK], BF16, name="hid%d" % h, align_bytes=ALIGN)
+            nc.vector.tensor_tensor(
+                hid[:].rearrange("p (c i s) -> p c s i", i=4, s=PACK),
+                first[:].rearrange("p s (c i) -> p c s i", i=4),
+                second[:, :, cols].rearrange("p s (c i) -> p c s i", i=4),
+                MAX,
+            )
+            hq = pool.tile([P, HO], U32, name="hq%d" % h, align_bytes=ALIGN)
+            hq_s = pool.tile([P, HO], U8, name="hq_s%d" % h, align_bytes=ALIGN)
+            nc.vector.quantize_mx(out=hq[:].bitcast(FP8X4), scales=hq_s[:], in_=hid[:])
+            accs = []
+            for b in range(N // P):
+                rows = slice(b * P, (b + 1) * P)
+                if h == 0:
+                    acc = acc_lo[:, b, :]
+                else:
+                    acc = psum.tile([P, HO], F32, name="acc_hi%d" % b)[:]
+                nc.tensor.matmul_mx(
+                    out=acc, lhsT=wb_w[:, rows].bitcast(FP4X4), lhsT_scale=wb_s[:, rows],
+                    rhs=hq[:].bitcast(FP8X4), rhs_scale=hq_s[:], start=True, stop=True,
+                )
+                accs.append(acc)
+            for b, acc in enumerate(accs):
+                if h == 1 and b == 1:
+                    nc.vector.tensor_copy(p_sb[b][:, cols], acc)
+                else:
+                    nc.scalar.copy(p_sb[b][:, cols], acc)
+
+        for b in range(N // P):
+            m0 = pool.tile([P, U], F32, name="m0_%d" % b)
+            fetch(m0[:], p_sb[b], l6[:], so_sb[:, b:b + 1])
+            nc.vector.tensor_copy(pages[b][:].indirect(l7[:]), m0[:])
+            nc.sync.dma_start(out[b * P:(b + 1) * P, :], pages[b][:])

@@ -54,13 +54,13 @@ def tile_picked_tokens_respelled_one_mixedpair_one_posted_kernel(
 
         ua_rows = ua.rearrange("(p t) f -> t p f", t=PACK)
         ua_sb = [pool.tile([P, F], F32, name="ua%d" % t, tag="ua%d" % t) for t in range(PACK)]
-        l2 = load_list(offs2, "l2")
-        ha_sb = load_factor(nc.scalar, ha, "ha_sb", "ha_sb")
         nc.sync.dma_start(ua_sb[0][:], ua_rows[0])
-        l3 = load_list(offs3, "l3")
+        ha_sb = load_factor(nc.scalar, ha, "ha_sb", "ha_sb")
         hb_sb = load_factor(nc.scalar, hb, "hb_sb", "hb_sb")
+        l2 = load_list(offs2, "l2")
         for t in range(1, PACK):
             nc.sync.dma_start(ua_sb[t][:], ua_rows[t])
+        l3 = load_list(offs3, "l3")
 
         xs_all = pool.tile([P, T], U8, name="xs_all", tag="xs_all", align_bytes=ALIGN)
         nc.vector.memset(xs_all[:].bitcast(I32), 0)
@@ -95,11 +95,12 @@ def tile_picked_tokens_respelled_one_mixedpair_one_posted_kernel(
         HR = R // 2
         HM = HR // PACK
         wcd = [pool.tile([P, G], F32, name="wcd%d" % t) for t in range(PACK)]
-        wc_lo = pool.tile([P, PACK, HR], BF16, name="wc_lo")
         for t in range(PACK):
             fetch(wcd[t][:], ua_sb[t], l2[:], ha_sb[:, t:t + 1])
+        wc_lo = pool.tile([P, PACK, HR], BF16, name="wc_lo", tag="ua%d" % (PACK - 1))
+        for t in range(PACK):
             fetch(wc_lo[:, t, :], wcd[t], entries(l3, 0, HR), hb_sb[:, t:t + 1])
-        wc_hi = pool.tile([P, PACK, HR], BF16, name="wc_hi", tag="ua%d" % (PACK - 1))
+        wc_hi = pool.tile([P, PACK, HR], BF16, name="wc_hi", tag="ha_sb")
         for t in range(PACK):
             fetch(wc_hi[:, t, :], wcd[t], entries(l3, HR, HR), hb_sb[:, t:t + 1])
 
@@ -119,12 +120,11 @@ def tile_picked_tokens_respelled_one_mixedpair_one_posted_kernel(
             quantize_wc(g_lo[:, s, :], s, 0)
 
         wc_hi_v = wc_hi[:].rearrange("p t (c i s) -> p s c t i", i=2, s=PACK)
-        g_hi = [pool.tile([P, HR], BF16, name="g_hi%d" % s, align_bytes=ALIGN) for s in range(PACK)]
         for pair in ((0, 1), (2, 3)):
             for s in pair:
-                nc.vector.tensor_copy(g_hi[s][:].rearrange("p (c i t) -> p c t i", i=2, t=PACK), wc_hi_v[:, s])
+                nc.vector.tensor_copy(g_lo[:, s, :].rearrange("p (c i t) -> p c t i", i=2, t=PACK), wc_hi_v[:, s])
             for s in pair:
-                quantize_wc(g_hi[s][:], s, 1)
+                quantize_wc(g_lo[:, s, :], s, 1)
 
         def product1(acc, s, cols):
             nc.tensor.matmul_mx(
@@ -157,7 +157,7 @@ def tile_picked_tokens_respelled_one_mixedpair_one_posted_kernel(
         acc_lo = psum.tile([P, N // P, HO], F32, name="acc_lo")
         for h, first in enumerate((first_lo, first_hi)):
             cols = slice(h * HO, (h + 1) * HO)
-            hid = pool.tile([P, HO * PACK], BF16, name="hid%d" % h, align_bytes=ALIGN)
+            hid = pool.tile([P, HO * PACK], BF16, name="hid%d" % h, tag="hid", align_bytes=ALIGN)
             nc.vector.tensor_tensor(
                 hid[:].rearrange("p (c i s) -> p c s i", i=4, s=PACK),
                 first[:].rearrange("p s (c i) -> p c s i", i=4),

@@ -62,6 +62,9 @@ def tile_picked_tokens_respelled_one_mixedpair_one_posted_kernel(
             nc.sync.dma_start(ua_sb[t][:], ua_rows[t])
         l3 = load_list(offs3, "l3")
 
+        warm = pool.tile([P, 2], F32, name="warm")
+        nc.vector.memset(warm[:, 0:1], 0.0)
+        nc.scalar.activation(out=warm[:, 1:2], in_=warm[:, 0:1], func=COPY)
         xs_all = pool.tile([P, T], U8, name="xs_all", tag="xs_all", align_bytes=ALIGN)
         nc.vector.memset(xs_all[:].bitcast(I32), 0)
         wb_s = pool.tile([P, N], U8, name="wb_s", align_bytes=ALIGN)

from contextlib import ExitStack

import concourse.mybir as mybir

K, J, R, T, F, G, O, N, U, E = 512, 512, 512, 2048, 2048, 1024, 256, 256, 128, 512
FLOPS = 2 * K * R * J + 2 * R * N * O

F32 = mybir.dt.float32
BF16 = mybir.dt.bfloat16
I32 = mybir.dt.int32
U32 = mybir.dt.uint32
U16 = mybir.dt.uint16
U8 = mybir.dt.uint8
FP8X4 = mybir.dt.float8_e4m3fn_x4
FP4X4 = mybir.dt.float4_e2m1fn_x4
COPY = mybir.ActivationFunctionType.Copy
MAX = mybir.AluOpType.max

P = 128
PACK = 4
LIST_ROWS = 16
ALIGN = 64


def tile_picked_tokens_respelled_one_mixedpair_one_posted_kernel(
    tc, xt_words, xt_scales, ua, ha, hb, sa, sb, wb_words, wb_scales, so,
    offs, offs2, offs3, offs4, offs5, offs6, offs7, out,
):
    nc = tc.nc
    with ExitStack() as ctx:
        lists = ctx.enter_context(tc.tile_pool(name="lists", bufs=1))
        pool = ctx.enter_context(tc.tile_pool(name="work", bufs=1))
        psum = ctx.enter_context(tc.psum_pool(name="psum", bufs=1))

        def load_list(src, name):
            t = lists.tile(list(src.shape), U16, name=name)
            nc.sync.dma_start(t[:], src)
            return t

        def load_factor(queue, src, name, tag):
            t = pool.tile([P, PACK], F32, name=name, tag=tag)
            queue.dma_start(t[:], src.rearrange("(p t) o -> p (t o)", t=PACK))
            return t

        def load_scale_rows(dst, src):
            for q in range(4):
                nc.sync.dma_start(dst[32 * q:32 * q + 4, :].bitcast(I32), src[0, 4 * q:4 * q + 4, :].bitcast(I32))

        def entries(lst, start, count):
            return lst[:, start // LIST_ROWS:(start + count) // LIST_ROWS]

        def fetch(dst, window, offsets, scale):
            nc.scalar.activation(out=dst, in_=window[:].indirect(offsets), func=COPY, scale=scale)

        ua_rows = ua.rearrange("(p t) f -> t p f", t=PACK)
        ua_sb = [pool.tile([P, F], F32, name="ua%d" % t, tag="ua%d" % t) for t in range(PACK)]
        nc.sync.dma_start(ua_sb[0][:], ua_rows[0])
        ha_sb = load_factor(nc.scalar, ha, "ha_sb", "ha_sb")
        hb_sb = load_factor(nc.scalar, hb, "hb_sb", "hb_sb")
        l2 = load_list(offs2, "l2")
        for t in range(1, PACK):
            nc.sync.dma_start(ua_sb[t][:], ua_rows[t])
        l3 = load_list(offs3, "l3")

        warm = pool.tile([P, 2], F32, name="warm")
        nc.vector.memset(warm[:, 0:1], 0.0)
        nc.scalar.activation(out=warm[:, 1:2], in_=warm[:, 0:1], func=COPY)
        xs_all = pool.tile([P, T], U8, name="xs_all", tag="xs_all", align_bytes=ALIGN)
        nc.vector.memset(xs_all[:].bitcast(I32), 0)
        wb_s = pool.tile([P, N], U8, name="wb_s", align_bytes=ALIGN)
        nc.vector.memset(wb_s[:].bitcast(I32), 0)
        pages = [pool.tile([P, E], F32, name="page%d" % b) for b in range(N // P)]
        for page in pages:
            nc.vector.memset(page[:], 0.0)

        xw_all = pool.tile([P, T], U16, name="xw_all")
        nc.sync.dma_start(xw_all[:].bitcast(I32), xt_words[0].bitcast(I32))
        l1 = load_list(offs, "l1")
        load_scale_rows(xs_all, xt_scales)
        sa_sb = load_factor(nc.sync, sa, "sa_sb", "sa_sb")
        l4 = load_list(offs4, "l4")
        sb_sb = load_factor(nc.sync, sb, "sb_sb", "sb_sb")
        l5 = load_list(offs5, "l5")
        wb_w = pool.tile([P, N], U16, name="wb_w", align_bytes=ALIGN)
        nc.sync.dma_start(wb_w[:].bitcast(I32), wb_words[0].bitcast(I32))
        load_scale_rows(wb_s, wb_scales)
        so_sb = pool.tile([P, N // P], F32, name="so_sb")
        with nc.allow_non_contiguous_dma(reason="one weight for each output feature, one feature a partition"):
            nc.sync.dma_start(so_sb[:], so.rearrange("(b p) o -> p (b o)", p=P))
        l6 = load_list(offs6, "l6")
        l7 = load_list(offs7, "l7")

        xw = pool.tile([P, J], U16, name="xw", align_bytes=ALIGN)
        nc.vector.tensor_copy(xw[:], xw_all[:].indirect(l1[:]))
        xs = pool.tile([P, J], U8, name="xs", align_bytes=ALIGN)
        nc.vector.tensor_copy(xs[:], xs_all[:].indirect(l1[:]))

        HR = R // 2
        HM = HR // PACK
        wcd = [pool.tile([P, G], F32, name="wcd%d" % t) for t in range(PACK)]
        for t in range(PACK):
            fetch(wcd[t][:], ua_sb[t], l2[:], ha_sb[:, t:t + 1])
        wc_lo = pool.tile([P, PACK, HR], BF16, name="wc_lo", tag="ua%d" % (PACK - 1))
        for t in range(PACK):
            fetch(wc_lo[:, t, :], wcd[t], entries(l3, 0, HR), hb_sb[:, t:t + 1])
        wc_hi = pool.tile([P, PACK, HR], BF16, name="wc_hi", tag="ha_sb")
        for t in range(PACK):
            fetch(wc_hi[:, t, :], wcd[t], entries(l3, HR, HR), hb_sb[:, t:t + 1])

        wq = [pool.tile([P, P], U32, name="wq%d" % s, align_bytes=ALIGN) for s in range(PACK)]
        wq_s = [pool.tile([P, P], U8, name="wq_s%d" % s, align_bytes=ALIGN) for s in range(PACK)]

        def quantize_wc(grouped, s, half):
            cols = slice(half * HM, (half + 1) * HM)
            nc.vector.quantize_mx(out=wq[s][:, cols].bitcast(FP8X4), scales=wq_s[s][:, cols], in_=grouped)

        g_lo = pool.tile([P, PACK, HR], BF16, name="g_lo", tag="xs_all", align_bytes=ALIGN)
        nc.vector.tensor_copy(
            g_lo[:].rearrange("p s (c i t) -> p c t i s", i=2, t=PACK),
            wc_lo[:].rearrange("p t (c i s) -> p c t i s", i=2, s=PACK),
        )
        for s in range(PACK):
            quantize_wc(g_lo[:, s, :], s, 0)

        wc_hi_v = wc_hi[:].rearrange("p t (c i s) -> p s c t i", i=2, s=PACK)
        for pair in ((0, 1), (2, 3)):
            for s in pair:
                nc.vector.tensor_copy(g_lo[:, s, :].rearrange("p (c i t) -> p c t i", i=2, t=PACK), wc_hi_v[:, s])
            for s in pair:
                quantize_wc(g_lo[:, s, :], s, 1)

        def product1(acc, s, cols):
            nc.tensor.matmul_mx(
                out=acc, lhsT=wq[s][:].bitcast(FP8X4), lhsT_scale=wq_s[s][:],
                rhs=xw[:, cols].bitcast(FP4X4), rhs_scale=xs[:, cols], start=True, stop=True,
            )

        a_sb = [pool.tile([P, J], F32, name="a%d" % s) for s in range(PACK)]
        for h in range(2):
            cols = slice(h * J // 2, (h + 1) * J // 2)
            acc = psum.tile([P, J // 2], F32, name="acc0_%d" % h)
            product1(acc[:], 0, cols)
            nc.scalar.copy(a_sb[0][:, cols], acc[:])
        for s in range(1, PACK):
            acc = psum.tile([P, J], F32, name="acc%d" % s)
            product1(acc[:], s, slice(0, J))
            nc.vector.tensor_copy(a_sb[s][:], acc[:])

        HO = O // 2
        first_lo = pool.tile([P, PACK, HO], F32, name="first_lo")
        second = pool.tile([P, PACK, O], F32, name="second")
        for s in range(PACK):
            fetch(first_lo[:, s, :], a_sb[s], entries(l4, 0, HO), sa_sb[:, s:s + 1])
            fetch(second[:, s, :], a_sb[s], l5[:], sb_sb[:, s:s + 1])
        first_hi = pool.tile([P, PACK, HO], F32, name="first_hi", tag="sb_sb")
        for s in range(PACK):
            fetch(first_hi[:, s, :], a_sb[s], entries(l4, HO, HO), sa_sb[:, s:s + 1])

        p_sb = [pool.tile([P, O], F32, name="p%d" % b) for b in range(N // P)]
        acc_lo = psum.tile([P, N // P, HO], F32, name="acc_lo")
        for h, first in enumerate((first_lo, first_hi)):
            cols = slice(h * HO, (h + 1) * HO)
            hid = pool.tile([P, HO * PACK], BF16, name="hid%d" % h, tag="hid", align_bytes=ALIGN)
            nc.vector.tensor_tensor(
                hid[:].rearrange("p (c i s) -> p c s i", i=4, s=PACK),
                first[:].rearrange("p s (c i) -> p c s i", i=4),
                second[:, :, cols].rearrange("p s (c i) -> p c s i", i=4),
                MAX,
            )
            hq = pool.tile([P, HO], U32, name="hq%d" % h, align_bytes=ALIGN)
            hq_s = pool.tile([P, HO], U8, name="hq_s%d" % h, align_bytes=ALIGN)
            nc.vector.quantize_mx(out=hq[:].bitcast(FP8X4), scales=hq_s[:], in_=hid[:])
            accs = []
            for b in range(N // P):
                rows = slice(b * P, (b + 1) * P)
                if h == 0:
                    acc = acc_lo[:, b, :]
                else:
                    acc = psum.tile([P, HO], F32, name="acc_hi%d" % b)[:]
                nc.tensor.matmul_mx(
                    out=acc, lhsT=wb_w[:, rows].bitcast(FP4X4), lhsT_scale=wb_s[:, rows],
                    rhs=hq[:].bitcast(FP8X4), rhs_scale=hq_s[:], start=True, stop=True,
                )
                accs.append(acc)
            for b, acc in enumerate(accs):
                if h == 1 and b == 1:
                    nc.vector.tensor_copy(p_sb[b][:, cols], acc)
                else:
                    nc.scalar.copy(p_sb[b][:, cols], acc)

        for b in range(N // P):
            m0 = pool.tile([P, U], F32, name="m0_%d" % b)
            fetch(m0[:], p_sb[b], l6[:], so_sb[:, b:b + 1])
            nc.vector.tensor_copy(pages[b][:].indirect(l7[:]), m0[:])
            nc.sync.dma_start(out[b * P:(b + 1) * P, :], pages[b][:])
